import numpy as np
import ml_dtypes


def mxq(x, axis, fmt="e4m3"):
    dtype, down = {"e4m3": (ml_dtypes.float8_e4m3fn, 7), "e5m2": (ml_dtypes.float8_e5m2, 14)}[fmt]
    v = np.moveaxis(np.asarray(x, np.float32).astype(ml_dtypes.bfloat16).astype(np.float64), axis, -1)
    blocks = v.reshape(v.shape[:-1] + (-1, 32))
    amax = np.abs(blocks).max(-1, keepdims=True)
    byte = np.maximum(np.where(amax > 0, np.frexp(amax)[1] - 1 + 127, 0) - down, 1)
    scale = np.exp2(byte - 127.0)
    codes = (blocks / scale).astype(np.float32).astype(dtype).astype(np.float64)
    return np.moveaxis((codes * scale).reshape(v.shape), -1, axis)


WIDE = False


def mx_kscale(k):
    if not WIDE:
        return np.ones(k)
    levels = np.array([30, -30])
    if k % 512:
        return np.exp2(np.random.permutation(np.resize(levels, k // 32))).repeat(32)
    a = np.empty((k // 512, 16))
    for p in range(k // 512):
        a[p, :8] = np.random.permutation(np.resize(levels, 8))
        for g in range(8):
            far = levels[np.abs(levels - a[p, g]) >= 10]
            a[p, g + 8] = far[np.random.randint(len(far))]
    return np.exp2(a.ravel()).repeat(32)


def f64(x):
    return np.asarray(x).astype(np.float64)


def striped(idx):
    return np.tile(np.asarray(idx).reshape(-1, 16).T, (8, 1)).astype(np.uint16)


def unstriped(offs):
    return offs[:16].T.reshape(-1).astype(np.int64)


E2M1 = np.array([0.0, 0.5, 1.0, 1.5, 2.0, 3.0, 4.0, 6.0, -0.0, -0.5, -1.0, -1.5, -2.0, -3.0, -4.0, -6.0])


def pack_weight(w, fmt):
    k, n = w.shape
    w = f64(np.asarray(w, np.float32).astype(ml_dtypes.bfloat16)).reshape(k // 32, 32, n)
    amax = np.abs(w).max(1)
    if fmt == "e4m3":
        byte = np.frexp(amax)[1] - 1 + 127 - 7
    else:
        mant, ex = np.frexp(amax / 6.0)
        byte = np.where(mant > 0.5, ex, ex - 1) + 127
    byte = np.clip(np.where(amax > 0, byte, 1), 1, 254)
    scaled = (w * np.exp2(127.0 - byte)[:, None, :]).reshape(k, n).astype(np.float32)
    by_word = np.ascontiguousarray(scaled.reshape(k // 512, 128, 4, n).transpose(0, 1, 3, 2))
    if fmt == "e4m3":
        words = by_word.astype(ml_dtypes.float8_e4m3fn).view(np.uint8)
    else:
        c = by_word.astype(ml_dtypes.float4_e2m1fn).view(np.uint8) & 0xF
        words = (c[..., 0::2] | (c[..., 1::2] << 4)).reshape(k // 512, 128, 2 * n)
    return np.ascontiguousarray(words), np.ascontiguousarray(byte.astype(np.uint8).reshape(k // 512, 16, n))


def unpack_weight(words, scales, fmt):
    g, _, n = scales.shape
    words = np.ascontiguousarray(words).reshape(g, 128, n, -1)
    if fmt == "e4m3":
        vals = words.view(ml_dtypes.float8_e4m3fn).astype(np.float64)
    else:
        nib = np.empty((g, 128, n, 4), np.uint8)
        nib[..., 0::2] = words & 0xF
        nib[..., 1::2] = words >> 4
        vals = E2M1[nib]
    vals = vals * np.repeat(np.exp2(scales.astype(np.float64) - 127.0), 8, axis=1)[..., None]
    return vals.transpose(0, 1, 3, 2).reshape(g * 512, n)


K, J, N, R, T, V, Q = 512, 512, 256, 256, 1024, 1024, 1024


def setup_inputs():
    n = np.random.standard_normal
    idx = np.random.permutation(T)[:J]
    idx2 = np.random.permutation(V)[:J]
    idx3 = np.random.permutation(Q)[:N]
    fj = mx_kscale(J)
    fk = mx_kscale(K)
    drp = pack_weight(n((K, R)) * 1 / np.sqrt(K) / fk[:, None], "e4m3")
    return {
        "xf": (n((K, T)) * np.random.uniform(0.4, 1.6, (1, T))).astype(np.float32),
        "ca": (np.random.uniform(0.5, 1.5, (J, 1)) * fj[:, None]).astype(np.float32),
        "gt": (n((N, V)) * np.exp(0.5 * n((1, V)))).astype(np.float32),
        "rb": (np.random.uniform(0.5, 1.5, (1, J)) / fj).astype(np.float32),
        "sv": (n((N, V))).astype(np.float32),
        "fkr": (np.random.uniform(0.5, 1.5, (1, K)) * fk).astype(np.float32),
        "dr_words": drp[0],
        "dr_scales": drp[1],
        "old": (0.5 * n((R, Q))).astype(np.float32),
        "offs": striped(idx),
        "offs2": striped(idx2),
        "offs3": striped(idx3),
    }


def reference(xf, ca, gt, rb, sv, fkr, dr_words, dr_scales, old, offs, offs2, offs3):
    idx = unstriped(offs)
    idx2 = unstriped(offs2)
    idx3 = unstriped(offs3)
    dru = unpack_weight(dr_words, dr_scales, "e4m3")
    xj = f64(xf)[:, idx].T
    uj = xj / (np.mean(np.abs(xj), axis=1, keepdims=True) + 0.1) * f64(ca) * f64(fkr)
    gs = f64(gt)[:, idx2] * np.maximum(f64(sv)[:, idx2], 0.0) * f64(rb)
    gj = gs.T
    ujq = mxq(uj, 0, "e4m3")
    gjq = mxq(gj, 0, "e5m2")
    w = ujq.T @ gjq
    wq = mxq(w, 0, "e5m2")
    v2 = dru.T @ wq
    wp = np.zeros((R, Q))
    wp[:, idx3] = v2
    y = 0.05 * wp + f64(old)
    return y

@@ -1,0 +1,274 @@
+from contextlib import ExitStack
+
+import concourse.mybir as mybir
+from concourse.masks import make_identity
+
+K, J, N, R, T, V, Q = 512, 512, 256, 256, 1024, 1024, 1024
+FLOPS = 2 * J * K * N + 2 * K * R * N
+
+F32 = mybir.dt.float32
+BF16 = mybir.dt.bfloat16
+I32 = mybir.dt.int32
+U32 = mybir.dt.uint32
+U16 = mybir.dt.uint16
+U8 = mybir.dt.uint8
+E4M3 = mybir.dt.float8_e4m3fn_x4
+E5M2 = mybir.dt.float8_e5m2_x4
+ALU = mybir.AluOpType
+ACT = mybir.ActivationFunctionType
+AXIS = mybir.AxisListType
+
+P = 128
+PACK = 4
+PER_COLUMN = 16
+X_ON_VECTOR = (512, 512, 512, 256)
+SCALE_ON = "SSVV"
+G_ON_VECTOR = (512, 0, 0, 0)
+U_ON_SCALAR = (2, 3)
+PRODUCT_ON_GPSIMD = ()
+STORE_WIDTHS = (512, 256, 256)
+
+
+def tile_list_directions_sized_saved_placed_kernel(
+    tc, xf, ca, gt, rb, sv, fkr, dr_words, dr_scales, old, offs, offs2, offs3, out
+):
+    nc = tc.nc
+    with ExitStack() as ctx:
+        lists = ctx.enter_context(tc.tile_pool(name="lists", bufs=1))
+        keep = ctx.enter_context(tc.tile_pool(name="keep", bufs=1))
+        psum = ctx.enter_context(tc.psum_pool(name="psum", bufs=1))
+
+        def bank(b, name):
+            return psum.tile([P, PACK, P], F32, name=name, tag="bank%d" % b)
+
+        def in_order(ap):
+            return ap.rearrange("p (q s) -> p q s", s=PACK)
+
+        def dealt(ap):
+            return ap.rearrange("p s q -> p q s")
+
+        def gather(dst, window, offsets, on_vector):
+            cut = on_vector // PER_COLUMN
+            if on_vector > 0:
+                nc.vector.tensor_copy(dst[:, 0:on_vector], window[:].indirect(offsets[:, 0:cut]))
+            if on_vector < J:
+                nc.scalar.activation(dst[:, on_vector:J], window[:].indirect(offsets[:, cut:]), ACT.Copy)
+
+        x_list = lists.tile([P, J // PER_COLUMN], U16, name="x_list")
+        g_list = lists.tile([P, J // PER_COLUMN], U16, name="g_list")
+        put_list = lists.tile([P, N // PER_COLUMN], U16, name="put_list")
+
+        x_rows = [keep.tile([P, T], F32, name="x_rows%d" % t) for t in range(PACK)]
+        sv_rows = [keep.tile([P, V], F32, name="sv_rows%d" % h) for h in range(2)]
+        gt_rows = [keep.tile([P, V], F32, name="gt_rows%d" % h) for h in range(2)]
+        old_rows = [keep.tile([P, Q], F32, name="old_rows%d" % r) for r in range(2)]
+        pages = [keep.tile([P, Q], F32, name="page%d" % r) for r in range(2)]
+        fk_cols = keep.tile([P, PACK], F32, name="fk_cols")
+        ca_cols = keep.tile([P, PACK], F32, name="ca_cols")
+        rb_cols = keep.tile([P, PACK], F32, name="rb_cols")
+        ident = keep.tile([P, P], F32, name="ident")
+        tenth = keep.tile([P, P], F32, name="tenth")
+        dr_codes = keep.tile([P, R], U32, name="dr_codes", align_bytes=64)
+        dr_plane = keep.tile([P, R], U8, name="dr_plane", align_bytes=64)
+
+        make_identity(nc, ident[:])
+        nc.gpsimd.tensor_scalar(tenth[:], ident[:], 0.0, 0.1 * K / P, ALU.mult, ALU.add)
+        nc.gpsimd.memset(dr_plane[:].bitcast(I32), 0)
+        for r in range(2):
+            nc.vector.memset(pages[r][:], 0.0)
+
+        x_planes = xf.rearrange("(p t) c -> t p c", t=PACK)
+        nc.sync.dma_start(x_list[:], offs)
+        nc.sync.dma_start(out=x_rows[0][:], in_=x_planes[0])
+        nc.sync.dma_start(out=fk_cols[:], in_=fkr[0].rearrange("(p t) -> p t", t=PACK))
+        for t in range(1, PACK):
+            nc.sync.dma_start(out=x_rows[t][:], in_=x_planes[t])
+        nc.sync.dma_start(g_list[:], offs2)
+        nc.sync.dma_start(out=sv_rows[0][:], in_=sv[0:P, :])
+        nc.sync.dma_start(out=ca_cols[:], in_=ca.rearrange("(p s) o -> p (s o)", s=PACK))
+        nc.sync.dma_start(out=gt_rows[0][:], in_=gt[0:P, :])
+        nc.sync.dma_start(out=rb_cols[:], in_=rb[0].rearrange("(p s) -> p s", s=PACK))
+        nc.sync.dma_start(out=sv_rows[1][:], in_=sv[P : 2 * P, :])
+        nc.sync.dma_start(out=gt_rows[1][:], in_=gt[P : 2 * P, :])
+        nc.sync.dma_start(
+            out=dr_codes[:].bitcast(I32),
+            in_=dr_words[0].rearrange("p n t -> p (n t)").bitcast(I32),
+        )
+        for q in range(4):
+            nc.sync.dma_start(
+                out=dr_plane[32 * q : 32 * q + 4, :].bitcast(I32),
+                in_=dr_scales[0, 4 * q : 4 * q + 4, :].bitcast(I32),
+            )
+        nc.sync.dma_start(put_list[:], offs3)
+        for r in range(2):
+            nc.sync.dma_start(out=old_rows[r][:], in_=old[r * P : (r + 1) * P, :])
+
+        abs_ps = bank(4, "abs_ps")
+        for s in range(PACK):
+            nc.tensor.matmul(abs_ps[:, s, :], tenth[:], ident[:], is_transpose=True, start=(s == 0), stop=False)
+        scaled = []
+        for t in range(PACK):
+            xg = keep.tile([P, J], F32, name="xg%d" % t)
+            gather(xg, x_rows[t], x_list, X_ON_VECTOR[t])
+            x_abs = keep.tile([P, PACK, P], F32, name="x_abs%d" % t)
+            nc.scalar.activation(dealt(x_abs[:]), in_order(xg[:]), ACT.Abs)
+            for s in range(PACK):
+                nc.tensor.matmul(
+                    abs_ps[:, s, :], x_abs[:, s, :], ident[:], is_transpose=True,
+                    start=False, stop=(t == PACK - 1 and s == PACK - 1),
+                )
+            x_scaled = keep.tile([P, PACK, P], F32, name="x_scaled%d" % t)
+            if SCALE_ON[t] == "V":
+                nc.vector.tensor_scalar(dealt(x_scaled[:]), in_order(xg[:]), fk_cols[:, t : t + 1], None, ALU.mult)
+            elif SCALE_ON[t] == "G":
+                nc.gpsimd.tensor_scalar(dealt(x_scaled[:]), in_order(xg[:]), fk_cols[:, t : t + 1], 0.0, ALU.mult, ALU.add)
+            else:
+                nc.scalar.activation(dealt(x_scaled[:]), in_order(xg[:]), ACT.Copy, scale=fk_cols[:, t : t + 1])
+            scaled.append(x_scaled)
+
+        xs_ps = []
+        for t in range(PACK):
+            xs_ps.append(bank(t, "xs_ps%d" % t))
+            for s in range(PACK):
+                nc.tensor.transpose(xs_ps[t][:, s, :], scaled[t][:, s, :], ident[:])
+
+        abs_sum = keep.tile([P, PACK], F32, name="abs_sum", tag="tie0", align_bytes=64)
+        nc.vector.tensor_reduce(abs_sum[:], abs_ps[:], AXIS.X, ALU.add)
+        inv_sum = keep.tile([P, PACK], F32, name="inv_sum")
+        nc.vector.reciprocal(inv_sum[:], abs_sum[:])
+        u_factor = keep.tile([P, PACK], F32, name="u_factor")
+        nc.vector.scalar_tensor_tensor(u_factor[:], inv_sum[:], float(K), ca_cols[:], ALU.mult, ALU.mult)
+        u_codes = keep.tile([P, K], U32, name="u_codes", align_bytes=64)
+        u_plane = keep.tile([P, K], U8, name="u_plane", align_bytes=64)
+        u16 = {}
+        g_ps = {}
+        g16 = {}
+        g_codes = [keep.tile([P, P], U32, name="g_codes%d" % h, align_bytes=64) for h in range(2)]
+        g_plane = [keep.tile([P, P], U8, name="g_plane%d" % h, align_bytes=64) for h in range(2)]
+        w16 = {}
+        w_codes = [keep.tile([P, P], U32, name="w_codes%d" % h, align_bytes=64) for h in range(2)]
+        w_plane = [keep.tile([P, P], U8, name="w_plane%d" % h, align_bytes=64) for h in range(2)]
+        picked = {}
+
+        def ue(t):
+            u16[t] = keep.tile([P, P, PACK], BF16, name="u16_%d" % t, tag=("tie1" if t == 0 else "u16_%d" % t), align_bytes=64)
+            if t in U_ON_SCALAR:
+                flat = keep.tile([P, PACK, P], BF16, name="u_flat%d" % t)
+                for s in range(PACK):
+                    nc.scalar.activation(flat[:, s, :], xs_ps[t][:, s, :], ACT.Copy, scale=u_factor[:, s : s + 1])
+                nc.vector.tensor_copy(
+                    u16[t][:].rearrange("p (c i) s -> p c s i", i=4), flat[:].rearrange("p s (c i) -> p c s i", i=4)
+                )
+            else:
+                nc.vector.tensor_tensor(
+                    u16[t][:], xs_ps[t][:].rearrange("p s m -> p m s"),
+                    u_factor[:].unsqueeze(1).to_broadcast([P, P, PACK]), ALU.mult,
+                )
+
+        def uq(t):
+            cols = slice(t * P, (t + 1) * P)
+            nc.vector.quantize_mx(
+                out=u_codes[:, cols].bitcast(E4M3), scales=u_plane[:, cols], in_=u16[t][:].rearrange("p m s -> p (m s)")
+            )
+
+        def gg(h):
+            svg = keep.tile([P, J], F32, name="svg%d" % h)
+            gtg = keep.tile([P, J], F32, name="gtg%d" % h)
+            gather(svg, sv_rows[h], g_list, G_ON_VECTOR[2 * h])
+            gather(gtg, gt_rows[h], g_list, G_ON_VECTOR[2 * h + 1])
+            picked[h] = (svg, gtg)
+
+        def gp(h):
+            svg, gtg = picked[h]
+            g_ps[h] = bank(5 + h, "g_ps%d" % h)
+            if h in PRODUCT_ON_GPSIMD:
+                g_prod = keep.tile([P, PACK, P], F32, name="g_prod%d" % h)
+                positive = keep.tile([P, J], F32, name="positive%d" % h)
+                nc.gpsimd.tensor_scalar(positive[:], svg[:], 0.0, 0.0, ALU.max, ALU.add)
+                nc.gpsimd.tensor_tensor(dealt(g_prod[:]), in_order(positive[:]), in_order(gtg[:]), ALU.mult)
+            else:
+                g_prod = keep.tile([P, PACK, P], F32, name="g_prod%d" % h, tag="tie%d" % h, align_bytes=64)
+                nc.vector.scalar_tensor_tensor(
+                    dealt(g_prod[:]), in_order(svg[:]), 0.0, in_order(gtg[:]), ALU.max, ALU.mult
+                )
+            for s in range(PACK):
+                nc.tensor.transpose(g_ps[h][:, s, :], g_prod[:, s, :], ident[:])
+
+        def ge(h):
+            g16[h] = keep.tile([P, P, PACK], BF16, name="g16_%d" % h, align_bytes=64)
+            nc.vector.tensor_tensor(
+                g16[h][:], g_ps[h][:].rearrange("p s n -> p n s"),
+                rb_cols[:].unsqueeze(1).to_broadcast([P, P, PACK]), ALU.mult,
+            )
+
+        def gq(h):
+            nc.vector.quantize_mx(
+                out=g_codes[h][:].bitcast(E5M2), scales=g_plane[h][:], in_=g16[h][:].rearrange("p n s -> p (n s)")
+            )
+
+        def w(h):
+            w_ps = bank(7 if h == 0 else 4, "w_ps%d" % h)
+            for t in range(PACK):
+                cols = slice(t * P, (t + 1) * P)
+                nc.tensor.matmul_mx(
+                    out=w_ps[:, t, :], lhsT=u_codes[:, cols].bitcast(E4M3), lhsT_scale=u_plane[:, cols],
+                    rhs=g_codes[h][:].bitcast(E5M2), rhs_scale=g_plane[h][:], start=True, stop=True,
+                )
+            w16[h] = keep.tile([P, P, PACK], BF16, name="w16_%d" % h, align_bytes=64)
+            if "SV"[h] == "S":
+                nc.scalar.copy(out=w16[h][:], in_=w_ps[:].rearrange("p t n -> p n t"))
+            else:
+                nc.vector.tensor_copy(out=w16[h][:], in_=w_ps[:].rearrange("p t n -> p n t"))
+
+        def wq(h):
+            nc.vector.quantize_mx(
+                out=w_codes[h][:].bitcast(E5M2), scales=w_plane[h][:], in_=w16[h][:].rearrange("p n t -> p (n t)")
+            )
+
+        def v(h):
+            places = put_list[:, h * (P // PER_COLUMN) : (h + 1) * (P // PER_COLUMN)]
+            for r in range(2):
+                cols = slice(r * P, (r + 1) * P)
+                v_ps = bank(2 * h + r, "v_ps%d%d" % (h, r))
+                nc.tensor.matmul_mx(
+                    out=v_ps[:, 0, :], lhsT=dr_codes[:, cols].bitcast(E4M3), lhsT_scale=dr_plane[:, cols],
+                    rhs=w_codes[h][:].bitcast(E5M2), rhs_scale=w_plane[h][:], start=True, stop=True,
+                )
+                v2 = keep.tile([P, P], F32, name="v2_%d%d" % (h, r))
+                if ("VS", "VS")[h][r] == "V":
+                    nc.vector.tensor_copy(out=v2[:], in_=v_ps[:, 0, :])
+                    nc.vector.tensor_copy(pages[r][:].indirect(places), v2[:])
+                else:
+                    nc.scalar.copy(out=v2[:], in_=v_ps[:, 0, :])
+                    nc.scalar.activation(pages[r][:].indirect(places), v2[:], ACT.Copy)
+
+        gg(0)
+        gp(0)
+        ue(0)
+        ge(0)
+        uq(0)
+        gg(1)
+        gp(1)
+        gq(0)
+        ue(1)
+        ge(1)
+        uq(1)
+        ue(2)
+        gq(1)
+        ue(3)
+        uq(2)
+        uq(3)
+        w(0)
+        w(1)
+        wq(0)
+        wq(1)
+        v(0)
+        v(1)
+        for r in range(2):
+            c0 = 0
+            for width in STORE_WIDTHS:
+                cols = slice(c0, c0 + width)
+                result = keep.tile([P, width], F32, name="result%d_%d" % (r, c0))
+                nc.vector.scalar_tensor_tensor(result[:], pages[r][:, cols], 0.05, old_rows[r][:, cols], ALU.mult, ALU.add)
+                nc.sync.dma_start(out=out[r * P : (r + 1) * P, cols], in_=result[:])
+                c0 = c0 + width

@@ -1,7 +1,6 @@
 from contextlib import ExitStack
 
 import concourse.mybir as mybir
-from concourse.masks import make_identity
 
 K, J, N, R, T, V, Q = 512, 512, 256, 256, 1024, 1024, 1024
 FLOPS = 2 * J * K * N + 2 * K * R * N
@@ -21,10 +20,10 @@ AXIS = mybir.AxisListType
 P = 128
 PACK = 4
 PER_COLUMN = 16
-X_ON_VECTOR = (512, 512, 512, 256)
-SCALE_ON = "SSVV"
-G_ON_VECTOR = (512, 0, 0, 0)
-U_ON_SCALAR = (2, 3)
+X_ON_VECTOR = (256, 256, 256, 256)
+SCALE_ON = "GGGV"
+G_ON_VECTOR = (256, 0, 0, 0)
+U_ON_SCALAR = ()
 PRODUCT_ON_GPSIMD = ()
 STORE_WIDTHS = (512, 256, 256)
 
@@ -46,6 +45,12 @@ def tile_list_directions_sized_saved_placed_kernel(
 
         def dealt(ap):
             return ap.rearrange("p s q -> p q s")
+
+        def lines_in(ap):
+            return ap.rearrange("p (c i s) -> p c s i", i=4, s=PACK)
+
+        def lines_out(ap):
+            return ap.rearrange("p s (c i) -> p c s i", i=4)
 
         def gather(dst, window, offsets, on_vector):
             cut = on_vector // PER_COLUMN
@@ -71,11 +76,20 @@ def tile_list_directions_sized_saved_placed_kernel(
         dr_codes = keep.tile([P, R], U32, name="dr_codes", align_bytes=64)
         dr_plane = keep.tile([P, R], U8, name="dr_plane", align_bytes=64)
 
-        make_identity(nc, ident[:])
-        nc.gpsimd.tensor_scalar(tenth[:], ident[:], 0.0, 0.1 * K / P, ALU.mult, ALU.add)
-        nc.gpsimd.memset(dr_plane[:].bitcast(I32), 0)
+        ones = keep.tile([P, P], F32, name="ones")
+        nc.vector.memset(ones[:], 1.0)
+        nc.scalar.activation(tenth[:], ones[:], ACT.Copy, scale=0.1 * K / P)
+        column = keep.tile([P, 32], F32, name="column", align_bytes=64)
+        row = keep.tile([P, 32], F32, name="row", align_bytes=64)
+        nc.vector.tensor_tensor_scan(column[:], ones[:, 0:32], ones[:, 0:32], 0.0, ALU.mult, ALU.add)
+        nc.vector.memset(ident[:], 0.0)
+        nc.vector.transpose(row[:], column[:])
+        nc.vector.memset(dr_plane[:].bitcast(I32), 0)
+        for q in range(4):
+            part = slice(32 * q, 32 * q + 32)
+            nc.vector.tensor_tensor(ident[part, part], column[part, :], row[part, :], ALU.is_equal)
         for r in range(2):
-            nc.vector.memset(pages[r][:], 0.0)
+            nc.gpsimd.memset(pages[r][:], 0.0)
 
         x_planes = xf.rearrange("(p t) c -> t p c", t=PACK)
         nc.sync.dma_start(x_list[:], offs)
@@ -111,7 +125,11 @@ def tile_list_directions_sized_saved_placed_kernel(
             xg = keep.tile([P, J], F32, name="xg%d" % t)
             gather(xg, x_rows[t], x_list, X_ON_VECTOR[t])
             x_abs = keep.tile([P, PACK, P], F32, name="x_abs%d" % t)
-            nc.scalar.activation(dealt(x_abs[:]), in_order(xg[:]), ACT.Abs)
+            cut = X_ON_VECTOR[t]
+            nc.vector.scalar_tensor_tensor(
+                dealt(x_abs[:, :, 0 : cut // PACK]), in_order(xg[:, 0:cut]), -1.0, in_order(xg[:, 0:cut]), ALU.mult, ALU.max
+            )
+            nc.scalar.activation(dealt(x_abs[:, :, cut // PACK : P]), in_order(xg[:, cut:J]), ACT.Abs)
             for s in range(PACK):
                 nc.tensor.matmul(
                     abs_ps[:, s, :], x_abs[:, s, :], ident[:], is_transpose=True,
@@ -121,7 +139,7 @@ def tile_list_directions_sized_saved_placed_kernel(
             if SCALE_ON[t] == "V":
                 nc.vector.tensor_scalar(dealt(x_scaled[:]), in_order(xg[:]), fk_cols[:, t : t + 1], None, ALU.mult)
             elif SCALE_ON[t] == "G":
-                nc.gpsimd.tensor_scalar(dealt(x_scaled[:]), in_order(xg[:]), fk_cols[:, t : t + 1], 0.0, ALU.mult, ALU.add)
+                nc.gpsimd.tensor_scalar(lines_out(x_scaled[:]), lines_in(xg[:]), fk_cols[:, t : t + 1], 0.0, ALU.mult, ALU.add)
             else:
                 nc.scalar.activation(dealt(x_scaled[:]), in_order(xg[:]), ACT.Copy, scale=fk_cols[:, t : t + 1])
             scaled.append(x_scaled)
@@ -151,8 +169,11 @@ def tile_list_directions_sized_saved_placed_kernel(
         picked = {}
 
         def ue(t):
-            u16[t] = keep.tile([P, P, PACK], BF16, name="u16_%d" % t, tag=("tie1" if t == 0 else "u16_%d" % t), align_bytes=64)
-            if t in U_ON_SCALAR:
+            u16[t] = keep.tile([P, P, PACK], BF16, name="u16_%d" % t, tag=("tie1" if t == 0 else "tie0" if t == 3 else "u16_%d" % t), align_bytes=64)
+            if t == 3:
+                for s in range(PACK):
+                    nc.scalar.activation(u16[t][:, :, s], xs_ps[t][:, s, :], ACT.Copy, scale=u_factor[:, s : s + 1])
+            elif t in U_ON_SCALAR:
                 flat = keep.tile([P, PACK, P], BF16, name="u_flat%d" % t)
                 for s in range(PACK):
                     nc.scalar.activation(flat[:, s, :], xs_ps[t][:, s, :], ACT.Copy, scale=u_factor[:, s : s + 1])
@@ -182,10 +203,10 @@ def tile_list_directions_sized_saved_placed_kernel(
             svg, gtg = picked[h]
             g_ps[h] = bank(5 + h, "g_ps%d" % h)
             if h in PRODUCT_ON_GPSIMD:
-                g_prod = keep.tile([P, PACK, P], F32, name="g_prod%d" % h)
+                g_prod = keep.tile([P, PACK, P], F32, name="g_prod%d" % h, tag="tie%d" % h, align_bytes=64)
                 positive = keep.tile([P, J], F32, name="positive%d" % h)
                 nc.gpsimd.tensor_scalar(positive[:], svg[:], 0.0, 0.0, ALU.max, ALU.add)
-                nc.gpsimd.tensor_tensor(dealt(g_prod[:]), in_order(positive[:]), in_order(gtg[:]), ALU.mult)
+                nc.gpsimd.tensor_tensor(lines_out(g_prod[:]), lines_in(positive[:]), lines_in(gtg[:]), ALU.mult)
             else:
                 g_prod = keep.tile([P, PACK, P], F32, name="g_prod%d" % h, tag="tie%d" % h, align_bytes=64)
                 nc.vector.scalar_tensor_tensor(
@@ -235,7 +256,7 @@ def tile_list_directions_sized_saved_placed_kernel(
                     rhs=w_codes[h][:].bitcast(E5M2), rhs_scale=w_plane[h][:], start=True, stop=True,
                 )
                 v2 = keep.tile([P, P], F32, name="v2_%d%d" % (h, r))
-                if ("VS", "VS")[h][r] == "V":
+                if ("SS", "VS")[h][r] == "V":
                     nc.vector.tensor_copy(out=v2[:], in_=v_ps[:, 0, :])
                     nc.vector.tensor_copy(pages[r][:].indirect(places), v2[:])
                 else:
@@ -245,24 +266,24 @@ def tile_list_directions_sized_saved_placed_kernel(
         gg(0)
         gp(0)
         ue(0)
+        ue(1)
         ge(0)
         uq(0)
         gg(1)
         gp(1)
         gq(0)
-        ue(1)
-        ge(1)
         uq(1)
         ue(2)
-        gq(1)
         ue(3)
         uq(2)
         uq(3)
         w(0)
-        w(1)
+        ge(1)
+        gq(1)
         wq(0)
-        wq(1)
+        w(1)
         v(0)
+        wq(1)
         v(1)
         for r in range(2):
             c0 = 0

@@ -22,7 +22,7 @@ PACK = 4
 PER_COLUMN = 16
 X_ON_VECTOR = (256, 256, 256, 256)
 SCALE_ON = "GGGV"
-G_ON_VECTOR = (256, 0, 0, 0)
+G_ON_VECTOR = (0, 0, 0, 0)
 U_ON_SCALAR = ()
 PRODUCT_ON_GPSIMD = ()
 STORE_WIDTHS = (512, 256, 256)
@@ -65,7 +65,7 @@ def tile_list_directions_sized_saved_placed_kernel(
 
         x_rows = [keep.tile([P, T], F32, name="x_rows%d" % t) for t in range(PACK)]
         sv_rows = [keep.tile([P, V], F32, name="sv_rows%d" % h) for h in range(2)]
-        gt_rows = [keep.tile([P, V], F32, name="gt_rows%d" % h) for h in range(2)]
+        gt_rows = [keep.tile([P, V], F32, name="gt_rows%d" % h, tag="gt_rows%d" % h) for h in range(2)]
         old_rows = [keep.tile([P, Q], F32, name="old_rows%d" % r) for r in range(2)]
         pages = [keep.tile([P, Q], F32, name="page%d" % r) for r in range(2)]
         fk_cols = keep.tile([P, PACK], F32, name="fk_cols")
@@ -89,7 +89,7 @@ def tile_list_directions_sized_saved_placed_kernel(
             part = slice(32 * q, 32 * q + 32)
             nc.vector.tensor_tensor(ident[part, part], column[part, :], row[part, :], ALU.is_equal)
         for r in range(2):
-            nc.gpsimd.memset(pages[r][:], 0.0)
+            nc.vector.memset(pages[r][:], 0.0)
 
         x_planes = xf.rearrange("(p t) c -> t p c", t=PACK)
         nc.sync.dma_start(x_list[:], offs)
@@ -120,11 +120,11 @@ def tile_list_directions_sized_saved_placed_kernel(
         abs_ps = bank(4, "abs_ps")
         for s in range(PACK):
             nc.tensor.matmul(abs_ps[:, s, :], tenth[:], ident[:], is_transpose=True, start=(s == 0), stop=False)
-        scaled = []
+        picked_x = []
         for t in range(PACK):
             xg = keep.tile([P, J], F32, name="xg%d" % t)
             gather(xg, x_rows[t], x_list, X_ON_VECTOR[t])
-            x_abs = keep.tile([P, PACK, P], F32, name="x_abs%d" % t)
+            x_abs = keep.tile([P, PACK, P], F32, name="x_abs%d" % t, tag="x_abs%d" % t)
             cut = X_ON_VECTOR[t]
             nc.vector.scalar_tensor_tensor(
                 dealt(x_abs[:, :, 0 : cut // PACK]), in_order(xg[:, 0:cut]), -1.0, in_order(xg[:, 0:cut]), ALU.mult, ALU.max
@@ -135,18 +135,18 @@ def tile_list_directions_sized_saved_placed_kernel(
                     abs_ps[:, s, :], x_abs[:, s, :], ident[:], is_transpose=True,
                     start=False, stop=(t == PACK - 1 and s == PACK - 1),
                 )
-            x_scaled = keep.tile([P, PACK, P], F32, name="x_scaled%d" % t)
-            if SCALE_ON[t] == "V":
-                nc.vector.tensor_scalar(dealt(x_scaled[:]), in_order(xg[:]), fk_cols[:, t : t + 1], None, ALU.mult)
-            elif SCALE_ON[t] == "G":
-                nc.gpsimd.tensor_scalar(lines_out(x_scaled[:]), lines_in(xg[:]), fk_cols[:, t : t + 1], 0.0, ALU.mult, ALU.add)
-            else:
-                nc.scalar.activation(dealt(x_scaled[:]), in_order(xg[:]), ACT.Copy, scale=fk_cols[:, t : t + 1])
-            scaled.append(x_scaled)
+            picked_x.append(xg)
 
-        xs_ps = []
+        early = keep.tile([P, PACK - 1, PACK, P], F32, name="x_scaled_early", tag="x_abs%d" % (PACK - 2))
+        last = keep.tile([P, PACK, P], F32, name="x_scaled_last")
+        scaled = [early[:, t] for t in range(PACK - 1)] + [last[:]]
         for t in range(PACK):
-            xs_ps.append(bank(t, "xs_ps%d" % t))
+            nc.vector.tensor_scalar(dealt(scaled[t]), in_order(picked_x[t][:]), fk_cols[:, t : t + 1], None, ALU.mult)
+
+        xs_ps = {}
+
+        def tx(t):
+            xs_ps[t] = bank(t, "xs_ps%d" % t)
             for s in range(PACK):
                 nc.tensor.transpose(xs_ps[t][:, s, :], scaled[t][:, s, :], ident[:])
 
@@ -168,32 +168,35 @@ def tile_list_directions_sized_saved_placed_kernel(
         w_plane = [keep.tile([P, P], U8, name="w_plane%d" % h, align_bytes=64) for h in range(2)]
         picked = {}
 
+        u_pairs = {}
+
         def ue(t):
-            u16[t] = keep.tile([P, P, PACK], BF16, name="u16_%d" % t, tag=("tie1" if t == 0 else "tie0" if t == 3 else "u16_%d" % t), align_bytes=64)
-            if t == 3:
-                for s in range(PACK):
-                    nc.scalar.activation(u16[t][:, :, s], xs_ps[t][:, s, :], ACT.Copy, scale=u_factor[:, s : s + 1])
-            elif t in U_ON_SCALAR:
-                flat = keep.tile([P, PACK, P], BF16, name="u_flat%d" % t)
+            if t % 2 == 0:
+                u_pairs[t // 2] = keep.tile([P, 2, P, PACK], BF16, name="u16_%d" % t, tag="svg%d" % (t // 2), align_bytes=64)
+            if t >= 2:
+                if t == 2:
+                    u_pairs["flat"] = keep.tile([P, 2, PACK, P], BF16, name="u_flat", tag="gt_rows1")
+                flat = u_pairs["flat"][:, t % 2]
                 for s in range(PACK):
                     nc.scalar.activation(flat[:, s, :], xs_ps[t][:, s, :], ACT.Copy, scale=u_factor[:, s : s + 1])
                 nc.vector.tensor_copy(
-                    u16[t][:].rearrange("p (c i) s -> p c s i", i=4), flat[:].rearrange("p s (c i) -> p c s i", i=4)
+                    u_pairs[1][:, t % 2].rearrange("p (c i) s -> p c s i", i=4), flat.rearrange("p s (c i) -> p c s i", i=4)
                 )
-            else:
-                nc.vector.tensor_tensor(
-                    u16[t][:], xs_ps[t][:].rearrange("p s m -> p m s"),
-                    u_factor[:].unsqueeze(1).to_broadcast([P, P, PACK]), ALU.mult,
-                )
+                return
+            nc.vector.tensor_tensor(
+                u_pairs[t // 2][:, t % 2], xs_ps[t][:].rearrange("p s m -> p m s"),
+                u_factor[:].unsqueeze(1).to_broadcast([P, P, PACK]), ALU.mult,
+            )
 
-        def uq(t):
-            cols = slice(t * P, (t + 1) * P)
+        def uQ(t):
+            cols = slice(t * P, (t + 2) * P)
             nc.vector.quantize_mx(
-                out=u_codes[:, cols].bitcast(E4M3), scales=u_plane[:, cols], in_=u16[t][:].rearrange("p m s -> p (m s)")
+                out=u_codes[:, cols].bitcast(E4M3), scales=u_plane[:, cols],
+                in_=u_pairs[t // 2][:].rearrange("p a m s -> p (a m s)"),
             )
 
         def gg(h):
-            svg = keep.tile([P, J], F32, name="svg%d" % h)
+            svg = keep.tile([P, J], F32, name="svg%d" % h, tag="svg%d" % h, align_bytes=64)
             gtg = keep.tile([P, J], F32, name="gtg%d" % h)
             gather(svg, sv_rows[h], g_list, G_ON_VECTOR[2 * h])
             gather(gtg, gt_rows[h], g_list, G_ON_VECTOR[2 * h + 1])
@@ -203,12 +206,12 @@ def tile_list_directions_sized_saved_placed_kernel(
             svg, gtg = picked[h]
             g_ps[h] = bank(5 + h, "g_ps%d" % h)
             if h in PRODUCT_ON_GPSIMD:
-                g_prod = keep.tile([P, PACK, P], F32, name="g_prod%d" % h, tag="tie%d" % h, align_bytes=64)
+                g_prod = keep.tile([P, PACK, P], F32, name="g_prod%d" % h, tag="tie0", align_bytes=64)
                 positive = keep.tile([P, J], F32, name="positive%d" % h)
                 nc.gpsimd.tensor_scalar(positive[:], svg[:], 0.0, 0.0, ALU.max, ALU.add)
                 nc.gpsimd.tensor_tensor(lines_out(g_prod[:]), lines_in(positive[:]), lines_in(gtg[:]), ALU.mult)
             else:
-                g_prod = keep.tile([P, PACK, P], F32, name="g_prod%d" % h, tag="tie%d" % h, align_bytes=64)
+                g_prod = keep.tile([P, PACK, P], F32, name="g_prod%d" % h, tag="tie0", align_bytes=64)
                 nc.vector.scalar_tensor_tensor(
                     dealt(g_prod[:]), in_order(svg[:]), 0.0, in_order(gtg[:]), ALU.max, ALU.mult
                 )
@@ -216,7 +219,7 @@ def tile_list_directions_sized_saved_placed_kernel(
                 nc.tensor.transpose(g_ps[h][:, s, :], g_prod[:, s, :], ident[:])
 
         def ge(h):
-            g16[h] = keep.tile([P, P, PACK], BF16, name="g16_%d" % h, align_bytes=64)
+            g16[h] = keep.tile([P, P, PACK], BF16, name="g16_%d" % h, tag=("svg1" if h else "g16"), align_bytes=64)
             nc.vector.tensor_tensor(
                 g16[h][:], g_ps[h][:].rearrange("p s n -> p n s"),
                 rb_cols[:].unsqueeze(1).to_broadcast([P, P, PACK]), ALU.mult,
@@ -263,20 +266,22 @@ def tile_list_directions_sized_saved_placed_kernel(
                     nc.scalar.copy(out=v2[:], in_=v_ps[:, 0, :])
                     nc.scalar.activation(pages[r][:].indirect(places), v2[:], ACT.Copy)
 
+        tx(0)
+        tx(1)
         gg(0)
         gp(0)
+        tx(2)
+        tx(3)
         ue(0)
         ue(1)
         ge(0)
-        uq(0)
+        uQ(0)
+        gq(0)
         gg(1)
         gp(1)
-        gq(0)
-        uq(1)
         ue(2)
         ue(3)
-        uq(2)
-        uq(3)
+        uQ(2)
         w(0)
         ge(1)
         gq(1)

@@ -94,9 +94,9 @@ def tile_list_directions_sized_saved_placed_kernel(
         x_planes = xf.rearrange("(p t) c -> t p c", t=PACK)
         nc.sync.dma_start(x_list[:], offs)
         nc.sync.dma_start(out=x_rows[0][:], in_=x_planes[0])
-        nc.sync.dma_start(out=fk_cols[:], in_=fkr[0].rearrange("(p t) -> p t", t=PACK))
         for t in range(1, PACK):
             nc.sync.dma_start(out=x_rows[t][:], in_=x_planes[t])
+        nc.sync.dma_start(out=fk_cols[:], in_=fkr[0].rearrange("(p t) -> p t", t=PACK))
         nc.sync.dma_start(g_list[:], offs2)
         nc.sync.dma_start(out=sv_rows[0][:], in_=sv[0:P, :])
         nc.sync.dma_start(out=ca_cols[:], in_=ca.rearrange("(p s) o -> p (s o)", s=PACK))
@@ -211,12 +211,10 @@ def tile_list_directions_sized_saved_placed_kernel(
                 nc.gpsimd.tensor_scalar(positive[:], svg[:], 0.0, 0.0, ALU.max, ALU.add)
                 nc.gpsimd.tensor_tensor(lines_out(g_prod[:]), lines_in(positive[:]), lines_in(gtg[:]), ALU.mult)
             else:
-                g_prod = keep.tile([P, PACK, P], F32, name="g_prod%d" % h, tag="tie0", align_bytes=64)
-                nc.vector.scalar_tensor_tensor(
-                    dealt(g_prod[:]), in_order(svg[:]), 0.0, in_order(gtg[:]), ALU.max, ALU.mult
-                )
+                g_prod = keep.tile([P, J], F32, name="g_prod%d" % h, tag="tie0", align_bytes=64)
+                nc.vector.scalar_tensor_tensor(g_prod[:], svg[:], 0.0, gtg[:], ALU.max, ALU.mult)
             for s in range(PACK):
-                nc.tensor.transpose(g_ps[h][:, s, :], g_prod[:, s, :], ident[:])
+                nc.tensor.transpose(g_ps[h][:, s, :], g_prod[:, s:J:PACK], ident[:])
 
         def ge(h):
             g16[h] = keep.tile([P, P, PACK], BF16, name="g16_%d" % h, tag=("svg1" if h else "g16"), align_bytes=64)

from contextlib import ExitStack

import concourse.mybir as mybir

K, J, N, R, T, V, Q = 512, 512, 256, 256, 1024, 1024, 1024
FLOPS = 2 * J * K * N + 2 * K * R * N

F32 = mybir.dt.float32
BF16 = mybir.dt.bfloat16
I32 = mybir.dt.int32
U32 = mybir.dt.uint32
U16 = mybir.dt.uint16
U8 = mybir.dt.uint8
E4M3 = mybir.dt.float8_e4m3fn_x4
E5M2 = mybir.dt.float8_e5m2_x4
ALU = mybir.AluOpType
ACT = mybir.ActivationFunctionType
AXIS = mybir.AxisListType

P = 128
PACK = 4
PER_COLUMN = 16
X_ON_VECTOR = (256, 256, 256, 256)
SCALE_ON = "GGGV"
G_ON_VECTOR = (0, 0, 0, 0)
U_ON_SCALAR = ()
PRODUCT_ON_GPSIMD = ()
STORE_WIDTHS = (512, 256, 256)


def tile_list_directions_sized_saved_placed_kernel(
    tc, xf, ca, gt, rb, sv, fkr, dr_words, dr_scales, old, offs, offs2, offs3, out
):
    nc = tc.nc
    with ExitStack() as ctx:
        lists = ctx.enter_context(tc.tile_pool(name="lists", bufs=1))
        keep = ctx.enter_context(tc.tile_pool(name="keep", bufs=1))
        psum = ctx.enter_context(tc.psum_pool(name="psum", bufs=1))

        def bank(b, name):
            return psum.tile([P, PACK, P], F32, name=name, tag="bank%d" % b)

        def in_order(ap):
            return ap.rearrange("p (q s) -> p q s", s=PACK)

        def dealt(ap):
            return ap.rearrange("p s q -> p q s")

        def lines_in(ap):
            return ap.rearrange("p (c i s) -> p c s i", i=4, s=PACK)

        def lines_out(ap):
            return ap.rearrange("p s (c i) -> p c s i", i=4)

        def gather(dst, window, offsets, on_vector):
            cut = on_vector // PER_COLUMN
            if on_vector > 0:
                nc.vector.tensor_copy(dst[:, 0:on_vector], window[:].indirect(offsets[:, 0:cut]))
            if on_vector < J:
                nc.scalar.activation(dst[:, on_vector:J], window[:].indirect(offsets[:, cut:]), ACT.Copy)

        x_list = lists.tile([P, J // PER_COLUMN], U16, name="x_list")
        g_list = lists.tile([P, J // PER_COLUMN], U16, name="g_list")
        put_list = lists.tile([P, N // PER_COLUMN], U16, name="put_list")

        x_rows = [keep.tile([P, T], F32, name="x_rows%d" % t) for t in range(PACK)]
        sv_rows = [keep.tile([P, V], F32, name="sv_rows%d" % h) for h in range(2)]
        gt_rows = [keep.tile([P, V], F32, name="gt_rows%d" % h, tag="gt_rows%d" % h) for h in range(2)]
        old_rows = [keep.tile([P, Q], F32, name="old_rows%d" % r) for r in range(2)]
        pages = [keep.tile([P, Q], F32, name="page%d" % r) for r in range(2)]
        fk_cols = keep.tile([P, PACK], F32, name="fk_cols")
        ca_cols = keep.tile([P, PACK], F32, name="ca_cols")
        rb_cols = keep.tile([P, PACK], F32, name="rb_cols")
        ident = keep.tile([P, P], F32, name="ident")
        tenth = keep.tile([P, P], F32, name="tenth")
        dr_codes = keep.tile([P, R], U32, name="dr_codes", align_bytes=64)
        dr_plane = keep.tile([P, R], U8, name="dr_plane", align_bytes=64)

        ones = keep.tile([P, P], F32, name="ones")
        nc.vector.memset(ones[:], 1.0)
        nc.scalar.activation(tenth[:], ones[:], ACT.Copy, scale=0.1 * K / P)
        column = keep.tile([P, 32], F32, name="column", align_bytes=64)
        row = keep.tile([P, 32], F32, name="row", align_bytes=64)
        nc.vector.tensor_tensor_scan(column[:], ones[:, 0:32], ones[:, 0:32], 0.0, ALU.mult, ALU.add)
        nc.vector.memset(ident[:], 0.0)
        nc.vector.transpose(row[:], column[:])
        nc.vector.memset(dr_plane[:].bitcast(I32), 0)
        for q in range(4):
            part = slice(32 * q, 32 * q + 32)
            nc.vector.tensor_tensor(ident[part, part], column[part, :], row[part, :], ALU.is_equal)
        for r in range(2):
            nc.vector.memset(pages[r][:], 0.0)

        x_planes = xf.rearrange("(p t) c -> t p c", t=PACK)
        nc.sync.dma_start(x_list[:], offs)
        nc.sync.dma_start(out=x_rows[0][:], in_=x_planes[0])
        for t in range(1, PACK):
            nc.sync.dma_start(out=x_rows[t][:], in_=x_planes[t])
        nc.sync.dma_start(out=fk_cols[:], in_=fkr[0].rearrange("(p t) -> p t", t=PACK))
        nc.sync.dma_start(g_list[:], offs2)
        nc.sync.dma_start(out=sv_rows[0][:], in_=sv[0:P, :])
        nc.sync.dma_start(out=ca_cols[:], in_=ca.rearrange("(p s) o -> p (s o)", s=PACK))
        nc.sync.dma_start(out=gt_rows[0][:], in_=gt[0:P, :])
        nc.sync.dma_start(out=rb_cols[:], in_=rb[0].rearrange("(p s) -> p s", s=PACK))
        nc.sync.dma_start(out=sv_rows[1][:], in_=sv[P : 2 * P, :])
        nc.sync.dma_start(out=gt_rows[1][:], in_=gt[P : 2 * P, :])
        nc.sync.dma_start(
            out=dr_codes[:].bitcast(I32),
            in_=dr_words[0].rearrange("p n t -> p (n t)").bitcast(I32),
        )
        for q in range(4):
            nc.sync.dma_start(
                out=dr_plane[32 * q : 32 * q + 4, :].bitcast(I32),
                in_=dr_scales[0, 4 * q : 4 * q + 4, :].bitcast(I32),
            )
        nc.sync.dma_start(put_list[:], offs3)
        for r in range(2):
            nc.sync.dma_start(out=old_rows[r][:], in_=old[r * P : (r + 1) * P, :])

        abs_ps = bank(4, "abs_ps")
        for s in range(PACK):
            nc.tensor.matmul(abs_ps[:, s, :], tenth[:], ident[:], is_transpose=True, start=(s == 0), stop=False)
        picked_x = []
        for t in range(PACK):
            xg = keep.tile([P, J], F32, name="xg%d" % t)
            gather(xg, x_rows[t], x_list, X_ON_VECTOR[t])
            x_abs = keep.tile([P, PACK, P], F32, name="x_abs%d" % t, tag="x_abs%d" % t)
            cut = X_ON_VECTOR[t]
            nc.vector.scalar_tensor_tensor(
                dealt(x_abs[:, :, 0 : cut // PACK]), in_order(xg[:, 0:cut]), -1.0, in_order(xg[:, 0:cut]), ALU.mult, ALU.max
            )
            nc.scalar.activation(dealt(x_abs[:, :, cut // PACK : P]), in_order(xg[:, cut:J]), ACT.Abs)
            for s in range(PACK):
                nc.tensor.matmul(
                    abs_ps[:, s, :], x_abs[:, s, :], ident[:], is_transpose=True,
                    start=False, stop=(t == PACK - 1 and s == PACK - 1),
                )
            picked_x.append(xg)

        early = keep.tile([P, PACK - 1, PACK, P], F32, name="x_scaled_early", tag="x_abs%d" % (PACK - 2))
        last = keep.tile([P, PACK, P], F32, name="x_scaled_last")
        scaled = [early[:, t] for t in range(PACK - 1)] + [last[:]]
        for t in range(PACK):
            nc.vector.tensor_scalar(dealt(scaled[t]), in_order(picked_x[t][:]), fk_cols[:, t : t + 1], None, ALU.mult)

        xs_ps = {}

        def tx(t):
            xs_ps[t] = bank(t, "xs_ps%d" % t)
            for s in range(PACK):
                nc.tensor.transpose(xs_ps[t][:, s, :], scaled[t][:, s, :], ident[:])

        abs_sum = keep.tile([P, PACK], F32, name="abs_sum", tag="tie0", align_bytes=64)
        nc.vector.tensor_reduce(abs_sum[:], abs_ps[:], AXIS.X, ALU.add)
        inv_sum = keep.tile([P, PACK], F32, name="inv_sum")
        nc.vector.reciprocal(inv_sum[:], abs_sum[:])
        u_factor = keep.tile([P, PACK], F32, name="u_factor")
        nc.vector.scalar_tensor_tensor(u_factor[:], inv_sum[:], float(K), ca_cols[:], ALU.mult, ALU.mult)
        u_codes = keep.tile([P, K], U32, name="u_codes", align_bytes=64)
        u_plane = keep.tile([P, K], U8, name="u_plane", align_bytes=64)
        u16 = {}
        g_ps = {}
        g16 = {}
        g_codes = [keep.tile([P, P], U32, name="g_codes%d" % h, align_bytes=64) for h in range(2)]
        g_plane = [keep.tile([P, P], U8, name="g_plane%d" % h, align_bytes=64) for h in range(2)]
        w16 = {}
        w_codes = [keep.tile([P, P], U32, name="w_codes%d" % h, align_bytes=64) for h in range(2)]
        w_plane = [keep.tile([P, P], U8, name="w_plane%d" % h, align_bytes=64) for h in range(2)]
        picked = {}

        u_pairs = {}

        def ue(t):
            if t % 2 == 0:
                u_pairs[t // 2] = keep.tile([P, 2, P, PACK], BF16, name="u16_%d" % t, tag="svg%d" % (t // 2), align_bytes=64)
            if t >= 2:
                if t == 2:
                    u_pairs["flat"] = keep.tile([P, 2, PACK, P], BF16, name="u_flat", tag="gt_rows1")
                flat = u_pairs["flat"][:, t % 2]
                for s in range(PACK):
                    nc.scalar.activation(flat[:, s, :], xs_ps[t][:, s, :], ACT.Copy, scale=u_factor[:, s : s + 1])
                nc.vector.tensor_copy(
                    u_pairs[1][:, t % 2].rearrange("p (c i) s -> p c s i", i=4), flat.rearrange("p s (c i) -> p c s i", i=4)
                )
                return
            nc.vector.tensor_tensor(
                u_pairs[t // 2][:, t % 2], xs_ps[t][:].rearrange("p s m -> p m s"),
                u_factor[:].unsqueeze(1).to_broadcast([P, P, PACK]), ALU.mult,
            )

        def uQ(t):
            cols = slice(t * P, (t + 2) * P)
            nc.vector.quantize_mx(
                out=u_codes[:, cols].bitcast(E4M3), scales=u_plane[:, cols],
                in_=u_pairs[t // 2][:].rearrange("p a m s -> p (a m s)"),
            )

        def gg(h):
            svg = keep.tile([P, J], F32, name="svg%d" % h, tag="svg%d" % h, align_bytes=64)
            gtg = keep.tile([P, J], F32, name="gtg%d" % h)
            gather(svg, sv_rows[h], g_list, G_ON_VECTOR[2 * h])
            gather(gtg, gt_rows[h], g_list, G_ON_VECTOR[2 * h + 1])
            picked[h] = (svg, gtg)

        def gp(h):
            svg, gtg = picked[h]
            g_ps[h] = bank(5 + h, "g_ps%d" % h)
            if h in PRODUCT_ON_GPSIMD:
                g_prod = keep.tile([P, PACK, P], F32, name="g_prod%d" % h, tag="tie0", align_bytes=64)
                positive = keep.tile([P, J], F32, name="positive%d" % h)
                nc.gpsimd.tensor_scalar(positive[:], svg[:], 0.0, 0.0, ALU.max, ALU.add)
                nc.gpsimd.tensor_tensor(lines_out(g_prod[:]), lines_in(positive[:]), lines_in(gtg[:]), ALU.mult)
            else:
                g_prod = keep.tile([P, J], F32, name="g_prod%d" % h, tag="tie0", align_bytes=64)
                nc.vector.scalar_tensor_tensor(g_prod[:], svg[:], 0.0, gtg[:], ALU.max, ALU.mult)
            for s in range(PACK):
                nc.tensor.transpose(g_ps[h][:, s, :], g_prod[:, s:J:PACK], ident[:])

        def ge(h):
            g16[h] = keep.tile([P, P, PACK], BF16, name="g16_%d" % h, tag=("svg1" if h else "g16"), align_bytes=64)
            nc.vector.tensor_tensor(
                g16[h][:], g_ps[h][:].rearrange("p s n -> p n s"),
                rb_cols[:].unsqueeze(1).to_broadcast([P, P, PACK]), ALU.mult,
            )

        def gq(h):
            nc.vector.quantize_mx(
                out=g_codes[h][:].bitcast(E5M2), scales=g_plane[h][:], in_=g16[h][:].rearrange("p n s -> p (n s)")
            )

        def w(h):
            w_ps = bank(7 if h == 0 else 4, "w_ps%d" % h)
            for t in range(PACK):
                cols = slice(t * P, (t + 1) * P)
                nc.tensor.matmul_mx(
                    out=w_ps[:, t, :], lhsT=u_codes[:, cols].bitcast(E4M3), lhsT_scale=u_plane[:, cols],
                    rhs=g_codes[h][:].bitcast(E5M2), rhs_scale=g_plane[h][:], start=True, stop=True,
                )
            w16[h] = keep.tile([P, P, PACK], BF16, name="w16_%d" % h, align_bytes=64)
            if "SV"[h] == "S":
                nc.scalar.copy(out=w16[h][:], in_=w_ps[:].rearrange("p t n -> p n t"))
            else:
                nc.vector.tensor_copy(out=w16[h][:], in_=w_ps[:].rearrange("p t n -> p n t"))

        def wq(h):
            nc.vector.quantize_mx(
                out=w_codes[h][:].bitcast(E5M2), scales=w_plane[h][:], in_=w16[h][:].rearrange("p n t -> p (n t)")
            )

        def v(h):
            places = put_list[:, h * (P // PER_COLUMN) : (h + 1) * (P // PER_COLUMN)]
            for r in range(2):
                cols = slice(r * P, (r + 1) * P)
                v_ps = bank(2 * h + r, "v_ps%d%d" % (h, r))
                nc.tensor.matmul_mx(
                    out=v_ps[:, 0, :], lhsT=dr_codes[:, cols].bitcast(E4M3), lhsT_scale=dr_plane[:, cols],
                    rhs=w_codes[h][:].bitcast(E5M2), rhs_scale=w_plane[h][:], start=True, stop=True,
                )
                v2 = keep.tile([P, P], F32, name="v2_%d%d" % (h, r))
                if ("SS", "VS")[h][r] == "V":
                    nc.vector.tensor_copy(out=v2[:], in_=v_ps[:, 0, :])
                    nc.vector.tensor_copy(pages[r][:].indirect(places), v2[:])
                else:
                    nc.scalar.copy(out=v2[:], in_=v_ps[:, 0, :])
                    nc.scalar.activation(pages[r][:].indirect(places), v2[:], ACT.Copy)

        tx(0)
        tx(1)
        gg(0)
        gp(0)
        tx(2)
        tx(3)
        ue(0)
        ue(1)
        ge(0)
        uQ(0)
        gq(0)
        gg(1)
        gp(1)
        ue(2)
        ue(3)
        uQ(2)
        w(0)
        ge(1)
        gq(1)
        wq(0)
        w(1)
        v(0)
        wq(1)
        v(1)
        for r in range(2):
            c0 = 0
            for width in STORE_WIDTHS:
                cols = slice(c0, c0 + width)
                result = keep.tile([P, width], F32, name="result%d_%d" % (r, c0))
                nc.vector.scalar_tensor_tensor(result[:], pages[r][:, cols], 0.05, old_rows[r][:, cols], ALU.mult, ALU.add)
                nc.sync.dma_start(out=out[r * P : (r + 1) * P, cols], in_=result[:])
                c0 = c0 + width
